import numpy as np
import ml_dtypes


def mxq(x, axis, fmt="e4m3"):
    dtype, down = {"e4m3": (ml_dtypes.float8_e4m3fn, 7), "e5m2": (ml_dtypes.float8_e5m2, 14)}[fmt]
    v = np.moveaxis(np.asarray(x, np.float32).astype(ml_dtypes.bfloat16).astype(np.float64), axis, -1)
    blocks = v.reshape(v.shape[:-1] + (-1, 32))
    amax = np.abs(blocks).max(-1, keepdims=True)
    byte = np.maximum(np.where(amax > 0, np.frexp(amax)[1] - 1 + 127, 0) - down, 1)
    scale = np.exp2(byte - 127.0)
    codes = (blocks / scale).astype(np.float32).astype(dtype).astype(np.float64)
    return np.moveaxis((codes * scale).reshape(v.shape), -1, axis)


WIDE = False


def mx_kscale(k):
    if not WIDE:
        return np.ones(k)
    levels = np.array([30, -30])
    if k % 512:
        return np.exp2(np.random.permutation(np.resize(levels, k // 32))).repeat(32)
    a = np.empty((k // 512, 16))
    for p in range(k // 512):
        a[p, :8] = np.random.permutation(np.resize(levels, 8))
        for g in range(8):
            far = levels[np.abs(levels - a[p, g]) >= 10]
            a[p, g + 8] = far[np.random.randint(len(far))]
    return np.exp2(a.ravel()).repeat(32)


def f64(x):
    return np.asarray(x).astype(np.float64)


def striped8(idx):
    return np.asarray(idx).reshape(8, -1, 16).transpose(0, 2, 1).reshape(128, -1).astype(np.uint16)


def unstriped8(offs):
    return offs.reshape(8, 16, -1).transpose(0, 2, 1).reshape(8, -1).astype(np.int64)


def pick8(x, idx, run):
    r = np.arange(len(x))
    return x[r[:, None], idx[r % (8 * run) // run]]


E2M1 = np.array([0.0, 0.5, 1.0, 1.5, 2.0, 3.0, 4.0, 6.0, -0.0, -0.5, -1.0, -1.5, -2.0, -3.0, -4.0, -6.0])


def pack_weight(w, fmt):
    k, n = w.shape
    w = f64(np.asarray(w, np.float32).astype(ml_dtypes.bfloat16)).reshape(k // 32, 32, n)
    amax = np.abs(w).max(1)
    if fmt in ("e4m3", "e5m2"):
        byte = np.frexp(amax)[1] - 1 + 127 - (7 if fmt == "e4m3" else 14)
    else:
        mant, ex = np.frexp(amax / 6.0)
        byte = np.where(mant > 0.5, ex, ex - 1) + 127
    byte = np.clip(np.where(amax > 0, byte, 1), 1, 254)
    scaled = (w * np.exp2(127.0 - byte)[:, None, :]).reshape(k, n).astype(np.float32)
    by_word = np.ascontiguousarray(scaled.reshape(k // 512, 128, 4, n).transpose(0, 1, 3, 2))
    if fmt in ("e4m3", "e5m2"):
        words = by_word.astype(ml_dtypes.float8_e4m3fn if fmt == "e4m3" else ml_dtypes.float8_e5m2).view(np.uint8)
    else:
        c = by_word.astype(ml_dtypes.float4_e2m1fn).view(np.uint8) & 0xF
        words = (c[..., 0::2] | (c[..., 1::2] << 4)).reshape(k // 512, 128, 2 * n)
    return np.ascontiguousarray(words), np.ascontiguousarray(byte.astype(np.uint8).reshape(k // 512, 16, n))


def unpack_weight(words, scales, fmt):
    g, _, n = scales.shape
    words = np.ascontiguousarray(words).reshape(g, 128, n, -1)
    if fmt in ("e4m3", "e5m2"):
        vals = words.view(ml_dtypes.float8_e4m3fn if fmt == "e4m3" else ml_dtypes.float8_e5m2).astype(np.float64)
    else:
        nib = np.empty((g, 128, n, 4), np.uint8)
        nib[..., 0::2] = words & 0xF
        nib[..., 1::2] = words >> 4
        vals = E2M1[nib]
    vals = vals * np.repeat(np.exp2(scales.astype(np.float64) - 127.0), 8, axis=1)[..., None]
    return vals.transpose(0, 1, 3, 2).reshape(g * 512, n)


def bf(x):
    return np.asarray(x, np.float32).astype(ml_dtypes.bfloat16)


def planes(Y):
    r, m = Y.shape
    b = f64(bf(Y)).reshape(r // 32, 32, m)
    amax = np.abs(b).max(1)
    byte = np.clip(np.where(amax > 0, np.frexp(amax)[1] - 1 + 127 - 7, 1), 1, 254)
    codes = (b * np.exp2(127.0 - byte)[:, None, :]).reshape(r, m).astype(np.float32).astype(ml_dtypes.float8_e4m3fn).view(np.uint8)
    words = codes.reshape(r // 512, 128, 4, m).transpose(0, 1, 3, 2)
    return np.ascontiguousarray(words), np.ascontiguousarray(byte.astype(np.uint8).reshape(r // 512, 16, m))


K, T, J, R, N = 1024, 512, 256, 512, 512


def setup_inputs():
    n = np.random.standard_normal
    idx = np.stack([np.random.permutation(T)[:J] for _ in range(8)])
    fk = mx_kscale(K)
    fr = mx_kscale(R)
    xtp = pack_weight(n((K, T)) / fk[:, None], "e5m2")
    wp = pack_weight(n((K, R)) * 1 / np.sqrt(K) * fk[:, None] * fr, "e4m3")
    wbp = pack_weight(n((R, N)) * 1 / np.sqrt(R) / fr[:, None], "e2m1")
    return {
        "xt_words": xtp[0],
        "xt_scales": xtp[1],
        "w_words": wp[0],
        "w_scales": wp[1],
        "us": (np.random.uniform(0.5, 2.0, (R, 1)) * fr[:, None]).astype(np.float32),
        "wb_words": wbp[0],
        "wb_scales": wbp[1],
        "rs": (n((N, J))).astype(np.float32),
        "gm": (np.random.uniform(0.5, 2.0, (N, 1))).astype(np.float32),
        "offs": striped8(idx),
    }


def reference(xt_words, xt_scales, w_words, w_scales, us, wb_words, wb_scales, rs, gm, offs):
    idx = unstriped8(offs)
    xtu = unpack_weight(xt_words, xt_scales, "e5m2")
    wu = unpack_weight(w_words, w_scales, "e4m3")
    wbu = unpack_weight(wb_words, wb_scales, "e2m1")
    xtidxg = pick8(xtu, idx, 64)
    a = wu.T @ xtidxg
    pk1 = np.max(np.abs(a), axis=1, keepdims=True)
    hid = a / pk1 * f64(us)
    hidq = mxq(hid, 0, "e5m2")
    p = wbu.T @ hidq
    y = f64(gm) * p + f64(rs)
    words, scales = planes(y)
    return y, words, scales

@@ -1,0 +1,186 @@
+from contextlib import ExitStack
+
+import concourse.mybir as mybir
+
+K, T, J, R, N = 1024, 512, 256, 512, 512
+FLOPS = 2 * K * R * J + 2 * R * N * J
+
+F32 = mybir.dt.float32
+BF16 = mybir.dt.bfloat16
+I32 = mybir.dt.int32
+U32 = mybir.dt.uint32
+U16 = mybir.dt.uint16
+U8 = mybir.dt.uint8
+E4M3 = mybir.dt.float8_e4m3fn_x4
+E5M2 = mybir.dt.float8_e5m2_x4
+E2M1 = mybir.dt.float4_e2m1fn_x4
+ALU = mybir.AluOpType
+
+P = 128
+PACK = 4
+PASSES = K // (P * PACK)
+HALF = J // 2
+
+
+def tile_list_headpicks_peakscaled_residual_pl_kernel(
+    tc, xt_words, xt_scales, w_words, w_scales, us, wb_words, wb_scales, rs, gm, offs, out_0, out_1, out_2
+):
+    nc = tc.nc
+    with ExitStack() as ctx:
+        pool = ctx.enter_context(tc.tile_pool(name="sbuf", bufs=1))
+        psum = ctx.enter_context(tc.psum_pool(name="psum", bufs=1))
+
+        def tile(shape, dtype, name, tag=None):
+            return pool.tile(shape, dtype, name=name, tag=tag or name, align_bytes=64)
+
+        lists = tile([P, J // 16], U16, "lists")
+        nc.sync.dma_start(lists[:], offs)
+
+        xs_window = [tile([P, T], U8, "xs_window%d" % z) for z in range(PASSES)]
+        for z in range(PASSES):
+            nc.vector.memset(xs_window[z][:].bitcast(I32), 0)
+            nc.scalar.dma_start(xs_window[z][0:P:8, :].bitcast(I32), xt_scales[z].bitcast(I32))
+
+        def load_words(src, name, tag=None):
+            words = tile([P, T], I32, name, tag)
+            nc.sync.dma_start(words[:], src.rearrange("p c b -> p (c b)").bitcast(I32))
+            return words
+
+        xw_window = [load_words(xt_words[0], "xw_window0")]
+        w_raw = [load_words(w_words[0], "w_raw0")]
+        ws_raw = tile([P, PASSES * R], U8, "ws_raw")
+        nc.vector.memset(ws_raw[:].bitcast(I32), 0)
+        for x in range(4):
+            nc.scalar.dma_start(
+                ws_raw[32 * x : 32 * x + 4, :].bitcast(I32).rearrange("p (z c) -> p z c", z=PASSES),
+                w_scales.bitcast(I32)[:, 4 * x : 4 * x + 4, :].rearrange("z q c -> q z c"),
+            )
+        us_sb = tile([P, PACK], F32, "us_sb")
+        nc.gpsimd.dma_start(us_sb[:], us.rearrange("(p t) o -> p (t o)", t=PACK))
+        gm_sb = tile([P, PACK], F32, "gm_sb")
+        nc.gpsimd.dma_start(gm_sb[:], gm.rearrange("(p t) o -> p (t o)", t=PACK))
+
+        xs_plane = tile([P, PASSES * J], U8, "xs_plane")
+        nc.vector.memset(xs_plane[:].bitcast(I32), 0)
+        xs_picked = tile([P, PASSES * J], U8, "xs_picked")
+        for z in range(PASSES):
+            nc.vector.tensor_copy(xs_picked[:, z * J : (z + 1) * J], xs_window[z][:].indirect(lists[:]))
+        for q in range(4):
+            queue = nc.sync if q % 2 == 0 else nc.scalar
+            queue.dma_start(xs_plane[q:P:32, :].bitcast(I32), xs_picked[8 * q : P : 32, :].bitcast(I32))
+        xw_window.append(load_words(xt_words[1], "xw_window1", "xs_window0"))
+        w_raw.append(load_words(w_words[1], "w_raw1", "xs_window1"))
+
+        xw_picked = [tile([P, J], U32, "xw_picked%d" % z) for z in range(PASSES)]
+        w_dealt = [tile([P, R], I32, "w_dealt%d" % z) for z in range(PASSES)]
+        ws_dealt = tile([P, PASSES * R], U8, "ws_dealt")
+        acc = [psum.tile([P, J], F32, name="acc%d" % t) for t in range(PACK)]
+        for z in range(PASSES):
+            nc.vector.tensor_copy(xw_picked[z][:], xw_window[z][:].bitcast(U32).indirect(lists[:]))
+            nc.vector.tensor_copy(
+                w_dealt[z][:].rearrange("p (t c i) -> p c t i", t=PACK, i=4),
+                w_raw[z][:].rearrange("p (c i t) -> p c t i", t=PACK, i=4),
+            )
+            if z == 0:
+                nc.vector.tensor_copy(
+                    ws_dealt[:].rearrange("p (t c i) -> p c t i", t=PACK, i=16),
+                    ws_raw[:].rearrange("p (c i t) -> p c t i", t=PACK, i=16),
+                )
+            for t in range(PACK):
+                lo = (t * PASSES + z) * P
+                nc.tensor.matmul_mx(
+                    out=acc[t][:],
+                    lhsT=w_dealt[z][:, t * P : (t + 1) * P].bitcast(E4M3),
+                    lhsT_scale=ws_dealt[:, lo : lo + P],
+                    rhs=xw_picked[z][:].bitcast(E5M2),
+                    rhs_scale=xs_plane[:, z * J : (z + 1) * J],
+                    start=(z == 0),
+                    stop=(z == PASSES - 1),
+                )
+
+        wbs_raw = tile([P, N], U8, "wbs_raw", tag="xw_window0")
+        nc.vector.memset(wbs_raw[:].bitcast(I32), 0)
+        for x in range(4):
+            nc.sync.dma_start(wbs_raw[32 * x : 32 * x + 4, :].bitcast(I32), wb_scales[0].bitcast(I32)[4 * x : 4 * x + 4, :])
+        wb_raw = tile([P, 2 * N], U8, "wb_raw", tag="w_raw0")
+        nc.sync.dma_start(wb_raw[:].bitcast(I32), wb_words[0].bitcast(I32))
+        rs_sb = tile([P, PACK * J], F32, "rs_sb", tag="xs_window0")
+        nc.sync.dma_start(rs_sb[:], rs.rearrange("(p t) j -> p (t j)", t=PACK))
+        wb_dealt = tile([P, 2 * N], U8, "wb_dealt", tag="ws_raw")
+        nc.vector.tensor_copy(
+            wb_dealt[:].rearrange("p (t c i b) -> p c t i b", t=PACK, i=8, b=2),
+            wb_raw[:].rearrange("p (c i t b) -> p c t i b", t=PACK, i=8, b=2),
+        )
+        wbs_dealt = tile([P, N], U8, "wbs_dealt")
+        nc.vector.tensor_copy(
+            wbs_dealt[:].rearrange("p (t c i) -> p c t i", t=PACK, i=16),
+            wbs_raw[:].rearrange("p (c i t) -> p c t i", t=PACK, i=16),
+        )
+
+        a_sb = [tile([P, J], F32, "a_sb%d" % t) for t in range(PACK)]
+        peak = [tile([P, 1], F32, "peak%d" % t) for t in range(PACK)]
+        inv_peak = [tile([P, 1], F32, "inv_peak%d" % t) for t in range(PACK)]
+        hid_rows = tile([P, PACK * J], BF16, "hid_rows")
+        for t in range(PACK):
+            nc.scalar.copy(a_sb[t][:], acc[t][:])
+            nc.vector.tensor_reduce(
+                peak[t][:], a_sb[t][:], axis=mybir.AxisListType.X, op=ALU.max, apply_absolute_value=True
+            )
+            nc.vector.reciprocal(inv_peak[t][:], peak[t][:])
+            nc.vector.tensor_scalar(
+                hid_rows[:, t * J : (t + 1) * J], a_sb[t][:], inv_peak[t][:], us_sb[:, t : t + 1], ALU.mult, ALU.mult
+            )
+
+        hid_woven = [tile([P, HALF * PACK], BF16, "hid_woven%d" % h) for h in range(2)]
+        hid_codes = [tile([P, HALF], U32, "hid_codes%d" % h) for h in range(2)]
+        hid_scales = [tile([P, HALF], U8, "hid_scales%d" % h) for h in range(2)]
+        prod = [psum.tile([P, PACK * HALF], F32, name="prod%d" % h) for h in range(2)]
+        y = [tile([P, PACK * HALF], F32, "y%d" % h) for h in range(2)]
+        y_woven = [tile([P, HALF * PACK], BF16, "y_woven%d" % h) for h in range(2)]
+        y_codes = tile([P, J], U32, "y_codes")
+        y_scales = tile([P, J], U8, "y_scales")
+        halves = [slice(h * HALF, (h + 1) * HALF) for h in range(2)]
+        for h in range(2):
+            nc.vector.tensor_copy(
+                hid_woven[h][:].rearrange("p (c i t) -> p c t i", t=PACK, i=4),
+                hid_rows[:].rearrange("p (t j) -> p t j", t=PACK)[:, :, halves[h]].rearrange("p t (c i) -> p c t i", i=4),
+            )
+        for h in range(2):
+            nc.vector.quantize_mx(out=hid_codes[h][:].bitcast(E5M2), scales=hid_scales[h][:], in_=hid_woven[h][:])
+            for t in range(PACK):
+                nc.tensor.matmul_mx(
+                    out=prod[h][:, t * HALF : (t + 1) * HALF],
+                    lhsT=wb_dealt[:, 2 * t * P : 2 * (t + 1) * P].bitcast(E2M1),
+                    lhsT_scale=wbs_dealt[:, t * P : (t + 1) * P],
+                    rhs=hid_codes[h][:].bitcast(E5M2),
+                    rhs_scale=hid_scales[h][:],
+                    start=True,
+                    stop=True,
+                )
+        for h in range(2):
+            for t in range(PACK):
+                nc.vector.scalar_tensor_tensor(
+                    y[h][:, t * HALF : (t + 1) * HALF],
+                    prod[h][:, t * HALF : (t + 1) * HALF],
+                    gm_sb[:, t : t + 1],
+                    rs_sb[:, t * J + h * HALF : t * J + (h + 1) * HALF],
+                    ALU.mult,
+                    ALU.add,
+                )
+            nc.sync.dma_start(
+                out_0.rearrange("(p t) j -> p t j", t=PACK)[:, :, halves[h]],
+                y[h][:].rearrange("p (t j) -> p t j", t=PACK),
+            )
+            weave = nc.scalar.copy if h == 0 else nc.vector.tensor_copy
+            weave(
+                y_woven[h][:].rearrange("p (c i t) -> p c t i", t=PACK, i=4),
+                y[h][:].rearrange("p (t c i) -> p c t i", t=PACK, i=4),
+            )
+        for h in range(2):
+            nc.vector.quantize_mx(
+                out=y_codes[:, halves[h]].bitcast(E4M3), scales=y_scales[:, halves[h]], in_=y_woven[h][:]
+            )
+        nc.sync.dma_start(out_1[0].rearrange("p c b -> p (c b)").bitcast(I32), y_codes[:].bitcast(I32))
+        for x in range(4):
+            queue = nc.scalar if x % 2 == 0 else nc.sync
+            queue.dma_start(out_2[0].bitcast(I32)[4 * x : 4 * x + 4, :], y_scales[32 * x : 32 * x + 4, :].bitcast(I32))

@@ -36,10 +36,14 @@ def tile_list_headpicks_peakscaled_residual_pl_kernel(
         lists = tile([P, J // 16], U16, "lists")
         nc.sync.dma_start(lists[:], offs)
 
-        xs_window = [tile([P, T], U8, "xs_window%d" % z) for z in range(PASSES)]
-        for z in range(PASSES):
-            nc.vector.memset(xs_window[z][:].bitcast(I32), 0)
-            nc.scalar.dma_start(xs_window[z][0:P:8, :].bitcast(I32), xt_scales[z].bitcast(I32))
+        us_sb = tile([P, PACK], F32, "us_sb")
+        nc.gpsimd.dma_start(us_sb[:], us.rearrange("(p t) o -> p (t o)", t=PACK))
+        gm_sb = tile([P, PACK], F32, "gm_sb")
+        nc.gpsimd.dma_start(gm_sb[:], gm.rearrange("(p t) o -> p (t o)", t=PACK))
+
+        xs_window = tile([P, T], U8, "xs_window")
+        nc.vector.memset(xs_window[:].bitcast(I32), 0)
+        nc.sync.dma_start(xs_window[0:P:4, :].bitcast(I32), xt_scales.bitcast(I32).rearrange("z q c -> q z c"))
 
         def load_words(src, name, tag=None):
             words = tile([P, T], I32, name, tag)
@@ -55,23 +59,21 @@ def tile_list_headpicks_peakscaled_residual_pl_kernel(
                 ws_raw[32 * x : 32 * x + 4, :].bitcast(I32).rearrange("p (z c) -> p z c", z=PASSES),
                 w_scales.bitcast(I32)[:, 4 * x : 4 * x + 4, :].rearrange("z q c -> q z c"),
             )
-        us_sb = tile([P, PACK], F32, "us_sb")
-        nc.gpsimd.dma_start(us_sb[:], us.rearrange("(p t) o -> p (t o)", t=PACK))
-        gm_sb = tile([P, PACK], F32, "gm_sb")
-        nc.gpsimd.dma_start(gm_sb[:], gm.rearrange("(p t) o -> p (t o)", t=PACK))
+        xw_window.append(load_words(xt_words[1], "xw_window1"))
+        w_raw.append(load_words(w_words[1], "w_raw1"))
 
         xs_plane = tile([P, PASSES * J], U8, "xs_plane")
         nc.vector.memset(xs_plane[:].bitcast(I32), 0)
-        xs_picked = tile([P, PASSES * J], U8, "xs_picked")
-        for z in range(PASSES):
-            nc.vector.tensor_copy(xs_picked[:, z * J : (z + 1) * J], xs_window[z][:].indirect(lists[:]))
-        for q in range(4):
-            queue = nc.sync if q % 2 == 0 else nc.scalar
-            queue.dma_start(xs_plane[q:P:32, :].bitcast(I32), xs_picked[8 * q : P : 32, :].bitcast(I32))
-        xw_window.append(load_words(xt_words[1], "xw_window1", "xs_window0"))
-        w_raw.append(load_words(w_words[1], "w_raw1", "xs_window1"))
+        xs_picked = tile([P, J], U8, "xs_picked")
+        nc.vector.tensor_copy(xs_picked[:], xs_window[:].indirect(lists[:]))
+        for x in range(4):
+            queue = nc.scalar if x % 2 == 0 else nc.sync
+            queue.dma_start(
+                xs_plane[32 * x : 32 * x + 4, :].bitcast(I32).rearrange("p (z c) -> p z c", z=PASSES),
+                xs_picked[32 * x : 32 * x + 32 : 4, :].bitcast(I32),
+            )
 
-        xw_picked = [tile([P, J], U32, "xw_picked%d" % z) for z in range(PASSES)]
+        xw_picked = [tile([P, J], U32, "xw_picked0"), tile([P, J], U32, "xw_picked1")]
         w_dealt = [tile([P, R], I32, "w_dealt%d" % z) for z in range(PASSES)]
         ws_dealt = tile([P, PASSES * R], U8, "ws_dealt")
         acc = [psum.tile([P, J], F32, name="acc%d" % t) for t in range(PACK)]
@@ -86,35 +88,30 @@ def tile_list_headpicks_peakscaled_residual_pl_kernel(
                     ws_dealt[:].rearrange("p (t c i) -> p c t i", t=PACK, i=16),
                     ws_raw[:].rearrange("p (c i t) -> p c t i", t=PACK, i=16),
                 )
-            for t in range(PACK):
-                lo = (t * PASSES + z) * P
-                nc.tensor.matmul_mx(
-                    out=acc[t][:],
-                    lhsT=w_dealt[z][:, t * P : (t + 1) * P].bitcast(E4M3),
-                    lhsT_scale=ws_dealt[:, lo : lo + P],
-                    rhs=xw_picked[z][:].bitcast(E5M2),
-                    rhs_scale=xs_plane[:, z * J : (z + 1) * J],
-                    start=(z == 0),
-                    stop=(z == PASSES - 1),
-                )
+        for z, t in [(0, 0), (0, 1), (1, 0), (1, 1), (0, 2), (1, 2), (0, 3), (1, 3)]:
+            lo = (t * PASSES + z) * P
+            nc.tensor.matmul_mx(
+                out=acc[t][:],
+                lhsT=w_dealt[z][:, t * P : (t + 1) * P].bitcast(E4M3),
+                lhsT_scale=ws_dealt[:, lo : lo + P],
+                rhs=xw_picked[z][:].bitcast(E5M2),
+                rhs_scale=xs_plane[:, z * J : (z + 1) * J],
+                start=(z == 0),
+                stop=(z == PASSES - 1),
+            )
 
-        wbs_raw = tile([P, N], U8, "wbs_raw", tag="xw_window0")
+        wb_raw = tile([P, 2 * N], U8, "wb_raw", tag="xw_window0")
+        nc.sync.dma_start(wb_raw[:].bitcast(I32), wb_words[0].bitcast(I32))
+        wbs_raw = tile([P, N], U8, "wbs_raw", tag="xs_window")
         nc.vector.memset(wbs_raw[:].bitcast(I32), 0)
         for x in range(4):
             nc.sync.dma_start(wbs_raw[32 * x : 32 * x + 4, :].bitcast(I32), wb_scales[0].bitcast(I32)[4 * x : 4 * x + 4, :])
-        wb_raw = tile([P, 2 * N], U8, "wb_raw", tag="w_raw0")
-        nc.sync.dma_start(wb_raw[:].bitcast(I32), wb_words[0].bitcast(I32))
-        rs_sb = tile([P, PACK * J], F32, "rs_sb", tag="xs_window0")
+        rs_sb = tile([P, PACK * J], F32, "rs_sb", tag="ws_raw")
         nc.sync.dma_start(rs_sb[:], rs.rearrange("(p t) j -> p (t j)", t=PACK))
-        wb_dealt = tile([P, 2 * N], U8, "wb_dealt", tag="ws_raw")
+        wb_dealt = tile([P, 2 * N], U8, "wb_dealt", tag="w_raw1")
         nc.vector.tensor_copy(
-            wb_dealt[:].rearrange("p (t c i b) -> p c t i b", t=PACK, i=8, b=2),
-            wb_raw[:].rearrange("p (c i t b) -> p c t i b", t=PACK, i=8, b=2),
-        )
-        wbs_dealt = tile([P, N], U8, "wbs_dealt")
-        nc.vector.tensor_copy(
-            wbs_dealt[:].rearrange("p (t c i) -> p c t i", t=PACK, i=16),
-            wbs_raw[:].rearrange("p (c i t) -> p c t i", t=PACK, i=16),
+            wb_dealt[:].bitcast(U16).rearrange("p (t c i) -> p c t i", t=PACK, i=8),
+            wb_raw[:].bitcast(U16).rearrange("p (c i t) -> p c t i", t=PACK, i=8),
         )
 
         a_sb = [tile([P, J], F32, "a_sb%d" % t) for t in range(PACK)]
@@ -130,6 +127,12 @@ def tile_list_headpicks_peakscaled_residual_pl_kernel(
             nc.vector.tensor_scalar(
                 hid_rows[:, t * J : (t + 1) * J], a_sb[t][:], inv_peak[t][:], us_sb[:, t : t + 1], ALU.mult, ALU.mult
             )
+
+        wbs_dealt = tile([P, N], U8, "wbs_dealt", tag="a_sb1")
+        nc.vector.tensor_copy(
+            wbs_dealt[:].rearrange("p (t c i) -> p c t i", t=PACK, i=16),
+            wbs_raw[:].rearrange("p (c i t) -> p c t i", t=PACK, i=16),
+        )
 
         hid_woven = [tile([P, HALF * PACK], BF16, "hid_woven%d" % h) for h in range(2)]
         hid_codes = [tile([P, HALF], U32, "hid_codes%d" % h) for h in range(2)]

@@ -36,13 +36,13 @@ def tile_list_headpicks_peakscaled_residual_pl_kernel(
         lists = tile([P, J // 16], U16, "lists")
         nc.sync.dma_start(lists[:], offs)
 
-        us_sb = tile([P, PACK], F32, "us_sb")
-        nc.gpsimd.dma_start(us_sb[:], us.rearrange("(p t) o -> p (t o)", t=PACK))
+        xs_window = tile([P, T], U8, "xs_window")
+        nc.vector.memset(xs_window[:].bitcast(I32), 0)
         gm_sb = tile([P, PACK], F32, "gm_sb")
         nc.gpsimd.dma_start(gm_sb[:], gm.rearrange("(p t) o -> p (t o)", t=PACK))
 
-        xs_window = tile([P, T], U8, "xs_window")
-        nc.vector.memset(xs_window[:].bitcast(I32), 0)
+        ws_raw = tile([P, PASSES * R], U8, "ws_raw")
+        nc.vector.memset(ws_raw[:].bitcast(I32), 0)
         nc.sync.dma_start(xs_window[0:P:4, :].bitcast(I32), xt_scales.bitcast(I32).rearrange("z q c -> q z c"))
 
         def load_words(src, name, tag=None):
@@ -51,9 +51,9 @@ def tile_list_headpicks_peakscaled_residual_pl_kernel(
             return words
 
         xw_window = [load_words(xt_words[0], "xw_window0")]
+        us_sb = tile([P, PACK], F32, "us_sb")
+        nc.sync.dma_start(us_sb[:], us.rearrange("(p t) o -> p (t o)", t=PACK))
         w_raw = [load_words(w_words[0], "w_raw0")]
-        ws_raw = tile([P, PASSES * R], U8, "ws_raw")
-        nc.vector.memset(ws_raw[:].bitcast(I32), 0)
         for x in range(4):
             nc.scalar.dma_start(
                 ws_raw[32 * x : 32 * x + 4, :].bitcast(I32).rearrange("p (z c) -> p z c", z=PASSES),
@@ -73,11 +73,12 @@ def tile_list_headpicks_peakscaled_residual_pl_kernel(
                 xs_picked[32 * x : 32 * x + 32 : 4, :].bitcast(I32),
             )
 
-        xw_picked = [tile([P, J], U32, "xw_picked0"), tile([P, J], U32, "xw_picked1")]
+        xw_picked = []
         w_dealt = [tile([P, R], I32, "w_dealt%d" % z) for z in range(PASSES)]
         ws_dealt = tile([P, PASSES * R], U8, "ws_dealt")
         acc = [psum.tile([P, J], F32, name="acc%d" % t) for t in range(PACK)]
         for z in range(PASSES):
+            xw_picked.append(tile([P, J], U32, "xw_picked%d" % z, tag="ws_raw" if z else None))
             nc.vector.tensor_copy(xw_picked[z][:], xw_window[z][:].bitcast(U32).indirect(lists[:]))
             nc.vector.tensor_copy(
                 w_dealt[z][:].rearrange("p (t c i) -> p c t i", t=PACK, i=4),
@@ -106,7 +107,7 @@ def tile_list_headpicks_peakscaled_residual_pl_kernel(
         nc.vector.memset(wbs_raw[:].bitcast(I32), 0)
         for x in range(4):
             nc.sync.dma_start(wbs_raw[32 * x : 32 * x + 4, :].bitcast(I32), wb_scales[0].bitcast(I32)[4 * x : 4 * x + 4, :])
-        rs_sb = tile([P, PACK * J], F32, "rs_sb", tag="ws_raw")
+        rs_sb = tile([P, PACK * J], F32, "rs_sb", tag="w_raw0")
         nc.sync.dma_start(rs_sb[:], rs.rearrange("(p t) j -> p (t j)", t=PACK))
         wb_dealt = tile([P, 2 * N], U8, "wb_dealt", tag="w_raw1")
         nc.vector.tensor_copy(
@@ -117,15 +118,25 @@ def tile_list_headpicks_peakscaled_residual_pl_kernel(
         a_sb = [tile([P, J], F32, "a_sb%d" % t) for t in range(PACK)]
         peak = [tile([P, 1], F32, "peak%d" % t) for t in range(PACK)]
         inv_peak = [tile([P, 1], F32, "inv_peak%d" % t) for t in range(PACK)]
-        hid_rows = tile([P, PACK * J], BF16, "hid_rows")
+        hid_rows = tile([P, 2 * J], BF16, "hid_rows")
+        hid_woven = [tile([P, HALF * PACK], BF16, "hid_woven%d" % h) for h in range(2)]
+        halves = [slice(h * HALF, (h + 1) * HALF) for h in range(2)]
         for t in range(PACK):
             nc.scalar.copy(a_sb[t][:], acc[t][:])
             nc.vector.tensor_reduce(
                 peak[t][:], a_sb[t][:], axis=mybir.AxisListType.X, op=ALU.max, apply_absolute_value=True
             )
             nc.vector.reciprocal(inv_peak[t][:], peak[t][:])
-            nc.vector.tensor_scalar(
-                hid_rows[:, t * J : (t + 1) * J], a_sb[t][:], inv_peak[t][:], us_sb[:, t : t + 1], ALU.mult, ALU.mult
+            factors = (inv_peak[t][:], us_sb[:, t : t + 1], ALU.mult, ALU.mult)
+            if t < 2:
+                nc.vector.tensor_scalar(hid_rows[:, t * J : (t + 1) * J], a_sb[t][:], *factors)
+            else:
+                for h in range(2):
+                    nc.vector.tensor_scalar(hid_woven[h][:, t : HALF * PACK : PACK], a_sb[t][:, halves[h]], *factors)
+        for h in range(2):
+            nc.scalar.copy(
+                hid_woven[h][:].rearrange("p (j t) -> p j t", t=PACK)[:, :, 0:2],
+                hid_rows[:].rearrange("p (t j) -> p j t", t=2)[:, halves[h], :],
             )
 
         wbs_dealt = tile([P, N], U8, "wbs_dealt", tag="a_sb1")
@@ -134,25 +145,21 @@ def tile_list_headpicks_peakscaled_residual_pl_kernel(
             wbs_raw[:].rearrange("p (c i t) -> p c t i", t=PACK, i=16),
         )
 
-        hid_woven = [tile([P, HALF * PACK], BF16, "hid_woven%d" % h) for h in range(2)]
         hid_codes = [tile([P, HALF], U32, "hid_codes%d" % h) for h in range(2)]
         hid_scales = [tile([P, HALF], U8, "hid_scales%d" % h) for h in range(2)]
-        prod = [psum.tile([P, PACK * HALF], F32, name="prod%d" % h) for h in range(2)]
+        prod = [
+            [psum.tile([P, HALF], F32, name="prod%d_%d" % (h, t), tag="acc%d" % t if h else "prod%d" % t) for t in range(PACK)]
+            for h in range(2)
+        ]
         y = [tile([P, PACK * HALF], F32, "y%d" % h) for h in range(2)]
         y_woven = [tile([P, HALF * PACK], BF16, "y_woven%d" % h) for h in range(2)]
         y_codes = tile([P, J], U32, "y_codes")
         y_scales = tile([P, J], U8, "y_scales")
-        halves = [slice(h * HALF, (h + 1) * HALF) for h in range(2)]
-        for h in range(2):
-            nc.vector.tensor_copy(
-                hid_woven[h][:].rearrange("p (c i t) -> p c t i", t=PACK, i=4),
-                hid_rows[:].rearrange("p (t j) -> p t j", t=PACK)[:, :, halves[h]].rearrange("p t (c i) -> p c t i", i=4),
-            )
         for h in range(2):
             nc.vector.quantize_mx(out=hid_codes[h][:].bitcast(E5M2), scales=hid_scales[h][:], in_=hid_woven[h][:])
             for t in range(PACK):
                 nc.tensor.matmul_mx(
-                    out=prod[h][:, t * HALF : (t + 1) * HALF],
+                    out=prod[h][t][:],
                     lhsT=wb_dealt[:, 2 * t * P : 2 * (t + 1) * P].bitcast(E2M1),
                     lhsT_scale=wbs_dealt[:, t * P : (t + 1) * P],
                     rhs=hid_codes[h][:].bitcast(E5M2),
@@ -164,7 +171,7 @@ def tile_list_headpicks_peakscaled_residual_pl_kernel(
             for t in range(PACK):
                 nc.vector.scalar_tensor_tensor(
                     y[h][:, t * HALF : (t + 1) * HALF],
-                    prod[h][:, t * HALF : (t + 1) * HALF],
+                    prod[h][t][:],
                     gm_sb[:, t : t + 1],
                     rs_sb[:, t * J + h * HALF : t * J + (h + 1) * HALF],
                     ALU.mult,
@@ -183,7 +190,9 @@ def tile_list_headpicks_peakscaled_residual_pl_kernel(
             nc.vector.quantize_mx(
                 out=y_codes[:, halves[h]].bitcast(E4M3), scales=y_scales[:, halves[h]], in_=y_woven[h][:]
             )
-        nc.sync.dma_start(out_1[0].rearrange("p c b -> p (c b)").bitcast(I32), y_codes[:].bitcast(I32))
+            nc.sync.dma_start(
+                out_1[0].rearrange("p c b -> p (c b)").bitcast(I32)[:, halves[h]], y_codes[:, halves[h]].bitcast(I32)
+            )
         for x in range(4):
             queue = nc.scalar if x % 2 == 0 else nc.sync
             queue.dma_start(out_2[0].bitcast(I32)[4 * x : 4 * x + 4, :], y_scales[32 * x : 32 * x + 4, :].bitcast(I32))

@@ -18,8 +18,20 @@ ALU = mybir.AluOpType
 
 P = 128
 PACK = 4
+QUAD = 32
+QUADS = P // QUAD
+ROWS = 4
+LINE = 16
 PASSES = K // (P * PACK)
-HALF = J // 2
+HALVES = 2
+HALF = J // HALVES
+
+
+def deal(nc, dst, src, run):
+    nc.vector.tensor_copy(
+        dst.rearrange("p (t c i) -> p c t i", t=PACK, i=run),
+        src.rearrange("p (c i t) -> p c t i", t=PACK, i=run),
+    )
 
 
 def tile_list_headpicks_peakscaled_residual_pl_kernel(
@@ -33,6 +45,9 @@ def tile_list_headpicks_peakscaled_residual_pl_kernel(
         def tile(shape, dtype, name, tag=None):
             return pool.tile(shape, dtype, name=name, tag=tag or name, align_bytes=64)
 
+        def live_rows(scale_tile, x):
+            return scale_tile[QUAD * x : QUAD * x + ROWS, :].bitcast(I32)
+
         lists = tile([P, J // 16], U16, "lists")
         nc.sync.dma_start(lists[:], offs)
 
@@ -45,8 +60,8 @@ def tile_list_headpicks_peakscaled_residual_pl_kernel(
         nc.vector.memset(ws_raw[:].bitcast(I32), 0)
         nc.sync.dma_start(xs_window[0:P:4, :].bitcast(I32), xt_scales.bitcast(I32).rearrange("z q c -> q z c"))
 
-        def load_words(src, name, tag=None):
-            words = tile([P, T], I32, name, tag)
+        def load_words(src, name):
+            words = tile([P, T], I32, name)
             nc.sync.dma_start(words[:], src.rearrange("p c b -> p (c b)").bitcast(I32))
             return words
 
@@ -54,23 +69,23 @@ def tile_list_headpicks_peakscaled_residual_pl_kernel(
         us_sb = tile([P, PACK], F32, "us_sb")
         nc.sync.dma_start(us_sb[:], us.rearrange("(p t) o -> p (t o)", t=PACK))
         w_raw = [load_words(w_words[0], "w_raw0")]
-        for x in range(4):
+        for x in range(QUADS):
             nc.scalar.dma_start(
-                ws_raw[32 * x : 32 * x + 4, :].bitcast(I32).rearrange("p (z c) -> p z c", z=PASSES),
-                w_scales.bitcast(I32)[:, 4 * x : 4 * x + 4, :].rearrange("z q c -> q z c"),
+                live_rows(ws_raw, x).rearrange("p (z c) -> p z c", z=PASSES),
+                w_scales.bitcast(I32)[:, ROWS * x : ROWS * (x + 1), :].rearrange("z q c -> q z c"),
             )
         xw_window.append(load_words(xt_words[1], "xw_window1"))
         w_raw.append(load_words(w_words[1], "w_raw1"))
 
-        xs_plane = tile([P, PASSES * J], U8, "xs_plane")
-        nc.vector.memset(xs_plane[:].bitcast(I32), 0)
+        xs_tile = tile([P, PASSES * J], U8, "xs_tile")
+        nc.vector.memset(xs_tile[:].bitcast(I32), 0)
         xs_picked = tile([P, J], U8, "xs_picked")
         nc.vector.tensor_copy(xs_picked[:], xs_window[:].indirect(lists[:]))
-        for x in range(4):
+        for x in range(QUADS):
             queue = nc.scalar if x % 2 == 0 else nc.sync
             queue.dma_start(
-                xs_plane[32 * x : 32 * x + 4, :].bitcast(I32).rearrange("p (z c) -> p z c", z=PASSES),
-                xs_picked[32 * x : 32 * x + 32 : 4, :].bitcast(I32),
+                live_rows(xs_tile, x).rearrange("p (z c) -> p z c", z=PASSES),
+                xs_picked[QUAD * x : QUAD * (x + 1) : 4, :].bitcast(I32),
             )
 
         xw_picked = []
@@ -80,23 +95,18 @@ def tile_list_headpicks_peakscaled_residual_pl_kernel(
         for z in range(PASSES):
             xw_picked.append(tile([P, J], U32, "xw_picked%d" % z, tag="ws_raw" if z else None))
             nc.vector.tensor_copy(xw_picked[z][:], xw_window[z][:].bitcast(U32).indirect(lists[:]))
-            nc.vector.tensor_copy(
-                w_dealt[z][:].rearrange("p (t c i) -> p c t i", t=PACK, i=4),
-                w_raw[z][:].rearrange("p (c i t) -> p c t i", t=PACK, i=4),
-            )
+            deal(nc, w_dealt[z][:], w_raw[z][:], LINE // 4)
             if z == 0:
-                nc.vector.tensor_copy(
-                    ws_dealt[:].rearrange("p (t c i) -> p c t i", t=PACK, i=16),
-                    ws_raw[:].rearrange("p (c i t) -> p c t i", t=PACK, i=16),
-                )
-        for z, t in [(0, 0), (0, 1), (1, 0), (1, 1), (0, 2), (1, 2), (0, 3), (1, 3)]:
+                deal(nc, ws_dealt[:], ws_raw[:], LINE)
+        order = [(z, t) for z in range(PASSES) for t in (0, 1)] + [(z, t) for t in (2, 3) for z in range(PASSES)]
+        for z, t in order:
             lo = (t * PASSES + z) * P
             nc.tensor.matmul_mx(
                 out=acc[t][:],
                 lhsT=w_dealt[z][:, t * P : (t + 1) * P].bitcast(E4M3),
                 lhsT_scale=ws_dealt[:, lo : lo + P],
                 rhs=xw_picked[z][:].bitcast(E5M2),
-                rhs_scale=xs_plane[:, z * J : (z + 1) * J],
+                rhs_scale=xs_tile[:, z * J : (z + 1) * J],
                 start=(z == 0),
                 stop=(z == PASSES - 1),
             )
@@ -105,22 +115,20 @@ def tile_list_headpicks_peakscaled_residual_pl_kernel(
         nc.sync.dma_start(wb_raw[:].bitcast(I32), wb_words[0].bitcast(I32))
         wbs_raw = tile([P, N], U8, "wbs_raw", tag="xs_window")
         nc.vector.memset(wbs_raw[:].bitcast(I32), 0)
-        for x in range(4):
-            nc.sync.dma_start(wbs_raw[32 * x : 32 * x + 4, :].bitcast(I32), wb_scales[0].bitcast(I32)[4 * x : 4 * x + 4, :])
+        for x in range(QUADS):
+            queue = nc.scalar if x < QUADS // 2 else nc.sync
+            queue.dma_start(live_rows(wbs_raw, x), wb_scales[0].bitcast(I32)[ROWS * x : ROWS * (x + 1), :])
         rs_sb = tile([P, PACK * J], F32, "rs_sb", tag="w_raw0")
         nc.sync.dma_start(rs_sb[:], rs.rearrange("(p t) j -> p (t j)", t=PACK))
         wb_dealt = tile([P, 2 * N], U8, "wb_dealt", tag="w_raw1")
-        nc.vector.tensor_copy(
-            wb_dealt[:].bitcast(U16).rearrange("p (t c i) -> p c t i", t=PACK, i=8),
-            wb_raw[:].bitcast(U16).rearrange("p (c i t) -> p c t i", t=PACK, i=8),
-        )
+        deal(nc, wb_dealt[:].bitcast(U16), wb_raw[:].bitcast(U16), LINE // 2)
 
         a_sb = [tile([P, J], F32, "a_sb%d" % t) for t in range(PACK)]
         peak = [tile([P, 1], F32, "peak%d" % t) for t in range(PACK)]
         inv_peak = [tile([P, 1], F32, "inv_peak%d" % t) for t in range(PACK)]
         hid_rows = tile([P, 2 * J], BF16, "hid_rows")
-        hid_woven = [tile([P, HALF * PACK], BF16, "hid_woven%d" % h) for h in range(2)]
-        halves = [slice(h * HALF, (h + 1) * HALF) for h in range(2)]
+        hid_woven = [tile([P, HALF * PACK], BF16, "hid_woven%d" % h) for h in range(HALVES)]
+        halves = [slice(h * HALF, (h + 1) * HALF) for h in range(HALVES)]
         for t in range(PACK):
             nc.scalar.copy(a_sb[t][:], acc[t][:])
             nc.vector.tensor_reduce(
@@ -130,32 +138,30 @@ def tile_list_headpicks_peakscaled_residual_pl_kernel(
             factors = (inv_peak[t][:], us_sb[:, t : t + 1], ALU.mult, ALU.mult)
             if t < 2:
                 nc.vector.tensor_scalar(hid_rows[:, t * J : (t + 1) * J], a_sb[t][:], *factors)
-            else:
-                for h in range(2):
+            if t == 1:
+                for h in range(HALVES):
+                    nc.scalar.copy(
+                        hid_woven[h][:].rearrange("p (j t) -> p j t", t=PACK)[:, :, 0:2],
+                        hid_rows[:].rearrange("p (t j) -> p j t", t=2)[:, halves[h], :],
+                    )
+            if t >= 2:
+                for h in range(HALVES):
                     nc.vector.tensor_scalar(hid_woven[h][:, t : HALF * PACK : PACK], a_sb[t][:, halves[h]], *factors)
-        for h in range(2):
-            nc.scalar.copy(
-                hid_woven[h][:].rearrange("p (j t) -> p j t", t=PACK)[:, :, 0:2],
-                hid_rows[:].rearrange("p (t j) -> p j t", t=2)[:, halves[h], :],
-            )
 
-        wbs_dealt = tile([P, N], U8, "wbs_dealt", tag="a_sb1")
-        nc.vector.tensor_copy(
-            wbs_dealt[:].rearrange("p (t c i) -> p c t i", t=PACK, i=16),
-            wbs_raw[:].rearrange("p (c i t) -> p c t i", t=PACK, i=16),
-        )
+        wbs_dealt = tile([P, N], U8, "wbs_dealt")
+        deal(nc, wbs_dealt[:], wbs_raw[:], LINE)
 
-        hid_codes = [tile([P, HALF], U32, "hid_codes%d" % h) for h in range(2)]
-        hid_scales = [tile([P, HALF], U8, "hid_scales%d" % h) for h in range(2)]
+        hid_codes = [tile([P, HALF], U32, "hid_codes%d" % h) for h in range(HALVES)]
+        hid_scales = [tile([P, HALF], U8, "hid_scales%d" % h) for h in range(HALVES)]
         prod = [
             [psum.tile([P, HALF], F32, name="prod%d_%d" % (h, t), tag="acc%d" % t if h else "prod%d" % t) for t in range(PACK)]
-            for h in range(2)
+            for h in range(HALVES)
         ]
-        y = [tile([P, PACK * HALF], F32, "y%d" % h) for h in range(2)]
-        y_woven = [tile([P, HALF * PACK], BF16, "y_woven%d" % h) for h in range(2)]
+        y = [tile([P, PACK * HALF], F32, "y%d" % h) for h in range(HALVES)]
+        y_woven = [tile([P, HALF * PACK], BF16, "y_woven%d" % h) for h in range(HALVES)]
         y_codes = tile([P, J], U32, "y_codes")
         y_scales = tile([P, J], U8, "y_scales")
-        for h in range(2):
+        for h in range(HALVES):
             nc.vector.quantize_mx(out=hid_codes[h][:].bitcast(E5M2), scales=hid_scales[h][:], in_=hid_woven[h][:])
             for t in range(PACK):
                 nc.tensor.matmul_mx(
@@ -167,7 +173,8 @@ def tile_list_headpicks_peakscaled_residual_pl_kernel(
                     start=True,
                     stop=True,
                 )
-        for h in range(2):
+
+        for h in range(HALVES):
             for t in range(PACK):
                 nc.vector.scalar_tensor_tensor(
                     y[h][:, t * HALF : (t + 1) * HALF],
@@ -183,16 +190,16 @@ def tile_list_headpicks_peakscaled_residual_pl_kernel(
             )
             weave = nc.scalar.copy if h == 0 else nc.vector.tensor_copy
             weave(
-                y_woven[h][:].rearrange("p (c i t) -> p c t i", t=PACK, i=4),
-                y[h][:].rearrange("p (t c i) -> p c t i", t=PACK, i=4),
+                y_woven[h][:].rearrange("p (c i t) -> p c t i", t=PACK, i=LINE // 4),
+                y[h][:].rearrange("p (t c i) -> p c t i", t=PACK, i=LINE // 4),
             )
-        for h in range(2):
+        for h in range(HALVES):
             nc.vector.quantize_mx(
                 out=y_codes[:, halves[h]].bitcast(E4M3), scales=y_scales[:, halves[h]], in_=y_woven[h][:]
             )
             nc.sync.dma_start(
                 out_1[0].rearrange("p c b -> p (c b)").bitcast(I32)[:, halves[h]], y_codes[:, halves[h]].bitcast(I32)
             )
-        for x in range(4):
+        for x in range(QUADS):
             queue = nc.scalar if x % 2 == 0 else nc.sync
-            queue.dma_start(out_2[0].bitcast(I32)[4 * x : 4 * x + 4, :], y_scales[32 * x : 32 * x + 4, :].bitcast(I32))
+            queue.dma_start(out_2[0].bitcast(I32)[ROWS * x : ROWS * (x + 1), :], live_rows(y_scales, x))

from contextlib import ExitStack

import concourse.mybir as mybir

K, T, J, R, N = 1024, 512, 256, 512, 512
FLOPS = 2 * K * R * J + 2 * R * N * J

F32 = mybir.dt.float32
BF16 = mybir.dt.bfloat16
I32 = mybir.dt.int32
U32 = mybir.dt.uint32
U16 = mybir.dt.uint16
U8 = mybir.dt.uint8
E4M3 = mybir.dt.float8_e4m3fn_x4
E5M2 = mybir.dt.float8_e5m2_x4
E2M1 = mybir.dt.float4_e2m1fn_x4
ALU = mybir.AluOpType

P = 128
PACK = 4
QUAD = 32
QUADS = P // QUAD
ROWS = 4
LINE = 16
PASSES = K // (P * PACK)
HALVES = 2
HALF = J // HALVES


def deal(nc, dst, src, run):
    nc.vector.tensor_copy(
        dst.rearrange("p (t c i) -> p c t i", t=PACK, i=run),
        src.rearrange("p (c i t) -> p c t i", t=PACK, i=run),
    )


def tile_list_headpicks_peakscaled_residual_pl_kernel(
    tc, xt_words, xt_scales, w_words, w_scales, us, wb_words, wb_scales, rs, gm, offs, out_0, out_1, out_2
):
    nc = tc.nc
    with ExitStack() as ctx:
        pool = ctx.enter_context(tc.tile_pool(name="sbuf", bufs=1))
        psum = ctx.enter_context(tc.psum_pool(name="psum", bufs=1))

        def tile(shape, dtype, name, tag=None):
            return pool.tile(shape, dtype, name=name, tag=tag or name, align_bytes=64)

        def live_rows(scale_tile, x):
            return scale_tile[QUAD * x : QUAD * x + ROWS, :].bitcast(I32)

        lists = tile([P, J // 16], U16, "lists")
        nc.sync.dma_start(lists[:], offs)

        xs_window = tile([P, T], U8, "xs_window")
        nc.vector.memset(xs_window[:].bitcast(I32), 0)
        gm_sb = tile([P, PACK], F32, "gm_sb")
        nc.gpsimd.dma_start(gm_sb[:], gm.rearrange("(p t) o -> p (t o)", t=PACK))

        ws_raw = tile([P, PASSES * R], U8, "ws_raw")
        nc.vector.memset(ws_raw[:].bitcast(I32), 0)
        nc.sync.dma_start(xs_window[0:P:4, :].bitcast(I32), xt_scales.bitcast(I32).rearrange("z q c -> q z c"))

        def load_words(src, name):
            words = tile([P, T], I32, name)
            nc.sync.dma_start(words[:], src.rearrange("p c b -> p (c b)").bitcast(I32))
            return words

        xw_window = [load_words(xt_words[0], "xw_window0")]
        us_sb = tile([P, PACK], F32, "us_sb")
        nc.sync.dma_start(us_sb[:], us.rearrange("(p t) o -> p (t o)", t=PACK))
        w_raw = [load_words(w_words[0], "w_raw0")]
        for x in range(QUADS):
            nc.scalar.dma_start(
                live_rows(ws_raw, x).rearrange("p (z c) -> p z c", z=PASSES),
                w_scales.bitcast(I32)[:, ROWS * x : ROWS * (x + 1), :].rearrange("z q c -> q z c"),
            )
        xw_window.append(load_words(xt_words[1], "xw_window1"))
        w_raw.append(load_words(w_words[1], "w_raw1"))

        xs_tile = tile([P, PASSES * J], U8, "xs_tile")
        nc.vector.memset(xs_tile[:].bitcast(I32), 0)
        xs_picked = tile([P, J], U8, "xs_picked")
        nc.vector.tensor_copy(xs_picked[:], xs_window[:].indirect(lists[:]))
        for x in range(QUADS):
            queue = nc.scalar if x % 2 == 0 else nc.sync
            queue.dma_start(
                live_rows(xs_tile, x).rearrange("p (z c) -> p z c", z=PASSES),
                xs_picked[QUAD * x : QUAD * (x + 1) : 4, :].bitcast(I32),
            )

        xw_picked = []
        w_dealt = [tile([P, R], I32, "w_dealt%d" % z) for z in range(PASSES)]
        ws_dealt = tile([P, PASSES * R], U8, "ws_dealt")
        acc = [psum.tile([P, J], F32, name="acc%d" % t) for t in range(PACK)]
        for z in range(PASSES):
            xw_picked.append(tile([P, J], U32, "xw_picked%d" % z, tag="ws_raw" if z else None))
            nc.vector.tensor_copy(xw_picked[z][:], xw_window[z][:].bitcast(U32).indirect(lists[:]))
            deal(nc, w_dealt[z][:], w_raw[z][:], LINE // 4)
            if z == 0:
                deal(nc, ws_dealt[:], ws_raw[:], LINE)
        order = [(z, t) for z in range(PASSES) for t in (0, 1)] + [(z, t) for t in (2, 3) for z in range(PASSES)]
        for z, t in order:
            lo = (t * PASSES + z) * P
            nc.tensor.matmul_mx(
                out=acc[t][:],
                lhsT=w_dealt[z][:, t * P : (t + 1) * P].bitcast(E4M3),
                lhsT_scale=ws_dealt[:, lo : lo + P],
                rhs=xw_picked[z][:].bitcast(E5M2),
                rhs_scale=xs_tile[:, z * J : (z + 1) * J],
                start=(z == 0),
                stop=(z == PASSES - 1),
            )

        wb_raw = tile([P, 2 * N], U8, "wb_raw", tag="xw_window0")
        nc.sync.dma_start(wb_raw[:].bitcast(I32), wb_words[0].bitcast(I32))
        wbs_raw = tile([P, N], U8, "wbs_raw", tag="xs_window")
        nc.vector.memset(wbs_raw[:].bitcast(I32), 0)
        for x in range(QUADS):
            queue = nc.scalar if x < QUADS // 2 else nc.sync
            queue.dma_start(live_rows(wbs_raw, x), wb_scales[0].bitcast(I32)[ROWS * x : ROWS * (x + 1), :])
        rs_sb = tile([P, PACK * J], F32, "rs_sb", tag="w_raw0")
        nc.sync.dma_start(rs_sb[:], rs.rearrange("(p t) j -> p (t j)", t=PACK))
        wb_dealt = tile([P, 2 * N], U8, "wb_dealt", tag="w_raw1")
        deal(nc, wb_dealt[:].bitcast(U16), wb_raw[:].bitcast(U16), LINE // 2)

        a_sb = [tile([P, J], F32, "a_sb%d" % t) for t in range(PACK)]
        peak = [tile([P, 1], F32, "peak%d" % t) for t in range(PACK)]
        inv_peak = [tile([P, 1], F32, "inv_peak%d" % t) for t in range(PACK)]
        hid_rows = tile([P, 2 * J], BF16, "hid_rows")
        hid_woven = [tile([P, HALF * PACK], BF16, "hid_woven%d" % h) for h in range(HALVES)]
        halves = [slice(h * HALF, (h + 1) * HALF) for h in range(HALVES)]
        for t in range(PACK):
            nc.scalar.copy(a_sb[t][:], acc[t][:])
            nc.vector.tensor_reduce(
                peak[t][:], a_sb[t][:], axis=mybir.AxisListType.X, op=ALU.max, apply_absolute_value=True
            )
            nc.vector.reciprocal(inv_peak[t][:], peak[t][:])
            factors = (inv_peak[t][:], us_sb[:, t : t + 1], ALU.mult, ALU.mult)
            if t < 2:
                nc.vector.tensor_scalar(hid_rows[:, t * J : (t + 1) * J], a_sb[t][:], *factors)
            if t == 1:
                for h in range(HALVES):
                    nc.scalar.copy(
                        hid_woven[h][:].rearrange("p (j t) -> p j t", t=PACK)[:, :, 0:2],
                        hid_rows[:].rearrange("p (t j) -> p j t", t=2)[:, halves[h], :],
                    )
            if t >= 2:
                for h in range(HALVES):
                    nc.vector.tensor_scalar(hid_woven[h][:, t : HALF * PACK : PACK], a_sb[t][:, halves[h]], *factors)

        wbs_dealt = tile([P, N], U8, "wbs_dealt")
        deal(nc, wbs_dealt[:], wbs_raw[:], LINE)

        hid_codes = [tile([P, HALF], U32, "hid_codes%d" % h) for h in range(HALVES)]
        hid_scales = [tile([P, HALF], U8, "hid_scales%d" % h) for h in range(HALVES)]
        prod = [
            [psum.tile([P, HALF], F32, name="prod%d_%d" % (h, t), tag="acc%d" % t if h else "prod%d" % t) for t in range(PACK)]
            for h in range(HALVES)
        ]
        y = [tile([P, PACK * HALF], F32, "y%d" % h) for h in range(HALVES)]
        y_woven = [tile([P, HALF * PACK], BF16, "y_woven%d" % h) for h in range(HALVES)]
        y_codes = tile([P, J], U32, "y_codes")
        y_scales = tile([P, J], U8, "y_scales")
        for h in range(HALVES):
            nc.vector.quantize_mx(out=hid_codes[h][:].bitcast(E5M2), scales=hid_scales[h][:], in_=hid_woven[h][:])
            for t in range(PACK):
                nc.tensor.matmul_mx(
                    out=prod[h][t][:],
                    lhsT=wb_dealt[:, 2 * t * P : 2 * (t + 1) * P].bitcast(E2M1),
                    lhsT_scale=wbs_dealt[:, t * P : (t + 1) * P],
                    rhs=hid_codes[h][:].bitcast(E5M2),
                    rhs_scale=hid_scales[h][:],
                    start=True,
                    stop=True,
                )

        for h in range(HALVES):
            for t in range(PACK):
                nc.vector.scalar_tensor_tensor(
                    y[h][:, t * HALF : (t + 1) * HALF],
                    prod[h][t][:],
                    gm_sb[:, t : t + 1],
                    rs_sb[:, t * J + h * HALF : t * J + (h + 1) * HALF],
                    ALU.mult,
                    ALU.add,
                )
            nc.sync.dma_start(
                out_0.rearrange("(p t) j -> p t j", t=PACK)[:, :, halves[h]],
                y[h][:].rearrange("p (t j) -> p t j", t=PACK),
            )
            weave = nc.scalar.copy if h == 0 else nc.vector.tensor_copy
            weave(
                y_woven[h][:].rearrange("p (c i t) -> p c t i", t=PACK, i=LINE // 4),
                y[h][:].rearrange("p (t c i) -> p c t i", t=PACK, i=LINE // 4),
            )
        for h in range(HALVES):
            nc.vector.quantize_mx(
                out=y_codes[:, halves[h]].bitcast(E4M3), scales=y_scales[:, halves[h]], in_=y_woven[h][:]
            )
            nc.sync.dma_start(
                out_1[0].rearrange("p c b -> p (c b)").bitcast(I32)[:, halves[h]], y_codes[:, halves[h]].bitcast(I32)
            )
        for x in range(QUADS):
            queue = nc.scalar if x % 2 == 0 else nc.sync
            queue.dma_start(out_2[0].bitcast(I32)[ROWS * x : ROWS * (x + 1), :], live_rows(y_scales, x))
